import numpy as np
import ml_dtypes


def mxq(x, axis, fmt="e4m3"):
    dtype, down = {"e4m3": (ml_dtypes.float8_e4m3fn, 7), "e5m2": (ml_dtypes.float8_e5m2, 14)}[fmt]
    v = np.moveaxis(np.asarray(x, np.float32).astype(ml_dtypes.bfloat16).astype(np.float64), axis, -1)
    blocks = v.reshape(v.shape[:-1] + (-1, 32))
    amax = np.abs(blocks).max(-1, keepdims=True)
    byte = np.maximum(np.where(amax > 0, np.frexp(amax)[1] - 1 + 127, 0) - down, 1)
    scale = np.exp2(byte - 127.0)
    codes = (blocks / scale).astype(np.float32).astype(dtype).astype(np.float64)
    return np.moveaxis((codes * scale).reshape(v.shape), -1, axis)


WIDE = False


def mx_kscale(k):
    if not WIDE:
        return np.ones(k)
    levels = np.array([10, -10, 5, -5, 0])
    if k % 512:
        return np.exp2(np.random.permutation(np.resize(levels, k // 32))).repeat(32)
    a = np.empty((k // 512, 16))
    for p in range(k // 512):
        a[p, :8] = np.random.permutation(np.resize(levels, 8))
        for g in range(8):
            far = levels[np.abs(levels - a[p, g]) >= 10]
            a[p, g + 8] = far[np.random.randint(len(far))]
    return np.exp2(a.ravel()).repeat(32)


def f64(x):
    return np.asarray(x).astype(np.float64)


def striped(idx):
    return np.tile(idx.reshape(-1, 16).T, (8, 1)).astype(np.uint16)


def unstriped(offs):
    return offs[:16].T.reshape(-1).astype(np.int64)


E2M1 = np.array([0.0, 0.5, 1.0, 1.5, 2.0, 3.0, 4.0, 6.0, -0.0, -0.5, -1.0, -1.5, -2.0, -3.0, -4.0, -6.0])


def pack_weight(w, fmt):
    k, n = w.shape
    w = f64(np.asarray(w, np.float32).astype(ml_dtypes.bfloat16)).reshape(k // 32, 32, n)
    amax = np.abs(w).max(1)
    if fmt == "e4m3":
        byte = np.frexp(amax)[1] - 1 + 127 - 7
    else:
        mant, ex = np.frexp(amax / 6.0)
        byte = np.where(mant > 0.5, ex, ex - 1) + 127
    byte = np.clip(np.where(amax > 0, byte, 1), 1, 254)
    scaled = (w * np.exp2(127.0 - byte)[:, None, :]).reshape(k, n).astype(np.float32)
    by_word = np.ascontiguousarray(scaled.reshape(k // 512, 128, 4, n).transpose(0, 1, 3, 2))
    if fmt == "e4m3":
        words = by_word.astype(ml_dtypes.float8_e4m3fn).view(np.uint8)
    else:
        c = by_word.astype(ml_dtypes.float4_e2m1fn).view(np.uint8) & 0xF
        words = (c[..., 0::2] | (c[..., 1::2] << 4)).reshape(k // 512, 128, 2 * n)
    return np.ascontiguousarray(words), np.ascontiguousarray(byte.astype(np.uint8).reshape(k // 512, 16, n))


def unpack_weight(words, scales, fmt):
    g, _, n = scales.shape
    words = np.ascontiguousarray(words).reshape(g, 128, n, -1)
    if fmt == "e4m3":
        vals = words.view(ml_dtypes.float8_e4m3fn).astype(np.float64)
    else:
        nib = np.empty((g, 128, n, 4), np.uint8)
        nib[..., 0::2] = words & 0xF
        nib[..., 1::2] = words >> 4
        vals = E2M1[nib]
    vals = vals * np.repeat(np.exp2(scales.astype(np.float64) - 127.0), 8, axis=1)[..., None]
    return vals.transpose(0, 1, 3, 2).reshape(g * 512, n)


def gelu(v):
    return 0.5 * v * (1.0 + np.tanh(np.sqrt(2.0 / np.pi) * (v + 0.044715 * v**3)))


def bf(x):
    return np.asarray(x, np.float32).astype(ml_dtypes.bfloat16)


def planes(Y):
    n, m = Y.shape
    b = f64(bf(Y)).reshape(n // 32, 32, m)
    amax = np.abs(b).max(1)
    byte = np.clip(np.where(amax > 0, np.frexp(amax)[1] - 1 + 127 - 7, 1), 1, 254)
    codes = (b * np.exp2(127.0 - byte)[:, None, :]).reshape(n, m).astype(np.float32).astype(ml_dtypes.float8_e4m3fn).view(np.uint8)
    words = codes.reshape(n // 512, 128, 4, m).transpose(0, 1, 3, 2)
    return np.ascontiguousarray(words), np.ascontiguousarray(byte.astype(np.uint8).reshape(n // 512, 16, m))


K, H, N, T, S, T2 = 1024, 512, 384, 2048, 1024, 2048

def setup_inputs():
    n = np.random.standard_normal
    s = mx_kscale(K)[:, None]
    u = mx_kscale(H)[:, None]
    tab_words, tab_scales = pack_weight(n((K, T)) * s, "e4m3")
    w1_words, w1_scales = pack_weight(n((K, H)) / np.sqrt(K) / s * u.T, "e2m1")
    w2 = (n((K, H)) / np.sqrt(K) / s * u.T).astype(np.float32)
    w3_words, w3_scales = pack_weight(n((K, H)) / np.sqrt(K) / s, "e4m3")
    w4_words, w4_scales = pack_weight(n((H, N)) / np.sqrt(H) / u, "e2m1")
    w5 = (n((H, N)) / np.sqrt(H) / u).astype(np.float32)
    return {"tab_words": tab_words, "tab_scales": tab_scales,
            "offs": striped(np.random.permutation(T)[:S]),
            "w1_words": w1_words, "w1_scales": w1_scales, "w2": w2,
            "w3_words": w3_words, "w3_scales": w3_scales,
            "page0": (n((H, T2)) * u).astype(np.float32),
            "offs2": striped(np.random.permutation(T2)[:S]),
            "wgs": np.exp(0.3 * n((128, S))).astype(np.float32),
            "w4_words": w4_words, "w4_scales": w4_scales, "w5": w5,
            "x0": n((N, T2)).astype(np.float32)}

def reference(tab_words, tab_scales, offs, w1_words, w1_scales, w2, w3_words, w3_scales,
              page0, offs2, wgs, w4_words, w4_scales, w5, x0):
    v = unpack_weight(tab_words, tab_scales, "e4m3")[:, unstriped(offs)]
    a = unpack_weight(w1_words, w1_scales, "e2m1").T @ v
    b = mxq(f64(w2), 0, "e4m3").T @ v
    c = unpack_weight(w3_words, w3_scales, "e4m3").T @ v
    h = np.minimum(a, b) * c
    page = f64(page0).copy()
    page[:, unstriped(offs2)] = np.tile(f64(wgs), (H // 128, 1)) * h
    words, scales = planes(page)
    pq = mxq(page, 0, "e4m3")
    d = unpack_weight(w4_words, w4_scales, "e2m1").T @ pq
    e = mxq(f64(w5), 0, "e4m3").T @ pq
    y = f64(x0) / (1.0 + np.exp(-d)) + e
    return y, page, words, scales

@@ -1,0 +1,390 @@
+from contextlib import ExitStack
+
+import concourse.mybir as mybir
+
+K, H, N, T, S, T2 = 1024, 512, 384, 2048, 1024, 2048
+FLOPS = 2 * (3 * K * H * S + 2 * H * N * T2)
+
+F32 = mybir.dt.float32
+BF16 = mybir.dt.bfloat16
+I32 = mybir.dt.int32
+U32 = mybir.dt.uint32
+U16 = mybir.dt.uint16
+U8 = mybir.dt.uint8
+FP8X4 = mybir.dt.float8_e4m3fn_x4
+FP4X4 = mybir.dt.float4_e2m1fn_x4
+MULT = mybir.AluOpType.mult
+MIN = mybir.AluOpType.min
+ADD = mybir.AluOpType.add
+SIGMOID = mybir.ActivationFunctionType.Sigmoid
+
+P = 128
+PACK = 4
+PASSES = K // (P * PACK)
+BANK = 512
+HALVES = S // BANK
+LIST_COLS = BANK // 16
+UNITS = [(t, h) for t in range(PACK) for h in range(HALVES)]
+EDGES = (0, 256, 512, 1024, 1536, 2048)
+CHUNKS = len(EDGES) - 1
+SPANS = [slice(EDGES[c], EDGES[c + 1]) for c in range(CHUNKS)]
+WIDTHS = [EDGES[c + 1] - EDGES[c] for c in range(CHUNKS)]
+NARROW = 2
+NT = N // P
+QUADS = 4
+
+
+def tile_list_cable_inspection_ledger_kernel(
+    tc, tab_words, tab_scales, offs, w1_words, w1_scales, w2, w3_words, w3_scales,
+    page0, offs2, wgs, w4_words, w4_scales, w5, x0, out_0, out_1, out_2, out_3,
+):
+    nc = tc.nc
+    with ExitStack() as ctx:
+        keep = ctx.enter_context(tc.tile_pool(name="keep", bufs=1))
+        ring = ctx.enter_context(tc.tile_pool(name="ring", bufs=3))
+        psum = ctx.enter_context(tc.psum_pool(name="psum", bufs=1))
+
+        def held(name, shape, dtype):
+            return keep.tile(shape, dtype, name=name, align_bytes=64)
+
+        tab_sc = held("tab_sc", [P, T], U8)
+        v_sc = held("v_sc", [P, S], U8)
+        v_sc_last = held("v_sc_last", [P, S], U8)
+        warm = held("warm", [P, 16], F32)
+        w13_sc_raw = held("w13_sc_raw", [P, PASSES * H], U8)
+        w4_sc = held("w4_sc", [P, N], U8)
+        nc.vector.memset(tab_sc[:].bitcast(I32), 0)
+        nc.gpsimd.memset(w13_sc_raw[:].bitcast(I32), 0)
+        nc.gpsimd.memset(w4_sc[:].bitcast(I32), 0)
+        nc.gpsimd.memset(v_sc_last[:].bitcast(I32), 0)
+        nc.gpsimd.memset(warm[:, 0:8], 0.0)
+        nc.scalar.activation(warm[:, 8:9], warm[:, 0:1], SIGMOID)
+
+        def load_scale_rows(queue, plane, first_row, src):
+            for q in range(QUADS):
+                row = 32 * q + first_row
+                queue.dma_start(
+                    out=plane[row : row + 4, :].bitcast(I32).rearrange("r (a y) -> r a y", a=src.shape[0]),
+                    in_=src[:, 4 * q : 4 * q + 4, :].rearrange("a r y -> r a y").bitcast(I32),
+                )
+
+        load_scale_rows(nc.gpsimd, w13_sc_raw, 0, w1_scales)
+
+        gather_list = held("gather_list", [P, S // 16], U16)
+        nc.sync.dma_start(gather_list[:], offs)
+        w3_raw = held("w3_raw", [P, PASSES * H], I32)
+        nc.sync.dma_start(
+            out=w3_raw[:].rearrange("p (a y) -> p a y", a=PASSES),
+            in_=w3_words.rearrange("a p y i -> p a (y i)").bitcast(I32),
+        )
+        for q in range(QUADS):
+            nc.sync.dma_start(
+                out=tab_sc[32 * q : 32 * q + 4 * PASSES, :].bitcast(I32),
+                in_=tab_scales[:, 4 * q : 4 * q + 4, :].bitcast(I32),
+            )
+        w1_raw = held("w1_raw", [P, PASSES * 2 * H], U8)
+        nc.sync.dma_start(
+            out=w1_raw[:].bitcast(I32).rearrange("p (a y) -> p a y", a=PASSES),
+            in_=w1_words.rearrange("a p y -> p a y").bitcast(I32),
+        )
+        w2_raw = [keep.tile([P, PACK, H], F32, name="w2_raw%d" % a, tag="wide%d" % a, align_bytes=64) for a in range(PASSES)]
+        tab_w = [held("tab_w%d" % a, [P, T], U32) for a in range(PASSES)]
+        for a in range(PASSES):
+            nc.sync.dma_start(out=w2_raw[a][:], in_=w2[512 * a : 512 * (a + 1), :].rearrange("(p j) y -> p j y", j=PACK))
+            if a == PASSES - 1:
+                load_scale_rows(nc.sync, w13_sc_raw, 4, w3_scales)
+            nc.sync.dma_start(out=tab_w[a][:].bitcast(I32), in_=tab_words[a].rearrange("p t i -> p (t i)").bitcast(I32))
+        scatter_list = held("scatter_list", [P, S // 16], U16)
+        nc.sync.dma_start(scatter_list[:], offs2)
+
+        wgs_rows = wgs.rearrange("(i t) j -> i t j", t=PACK)
+        wgs_first = keep.tile([P, S], F32, name="wgs_first", tag="first", align_bytes=64)
+        wgs_rest = held("wgs_rest", [P, PACK - 1, S], F32)
+        page_in = page0.rearrange("(p t) m -> t p m", t=PACK)
+        page_out = out_1.rearrange("(p t) m -> t p m", t=PACK)
+        page = [held("page%d" % t, [P, T2], F32) for t in range(PACK)]
+        for q in (0, 2, 1, 3):
+            nc.sync.dma_start(out=wgs_first[32 * q : 32 * (q + 1), :], in_=wgs_rows[:, 0, :])
+        nc.sync.dma_start(out=page[0][:], in_=page_in[0])
+        for q in (0, 2, 1, 3):
+            nc.sync.dma_start(out=wgs_rest[32 * q : 32 * (q + 1), :, :], in_=wgs_rows[:, 1:PACK, :])
+        nc.sync.dma_start(out=page[1][:], in_=page_in[1])
+        w5_raw = held("w5_raw", [P, PACK, N], F32)
+        nc.sync.dma_start(out=w5_raw[:], in_=w5.rearrange("(p j) n -> p j n", j=PACK))
+        w4_w = held("w4_w", [P, 2 * N], U8)
+        nc.sync.dma_start(out=w4_w[:].bitcast(I32), in_=w4_words[0].bitcast(I32))
+        load_scale_rows(nc.sync, w4_sc, 0, w4_scales)
+        for t in range(2, PACK):
+            nc.sync.dma_start(out=page[t][:], in_=page_in[t])
+
+        v_w = [[held("v_w%d%d" % (a, h), [P, BANK], U32) for h in range(HALVES)] for a in range(PASSES)]
+
+        def gather_words(a, h):
+            part = gather_list[:, LIST_COLS * h : LIST_COLS * (h + 1)]
+            nc.vector.tensor_copy(v_w[a][h][:], tab_w[a][:].indirect(part))
+
+        nc.vector.tensor_copy(v_sc[:], tab_sc[:].indirect(gather_list[:]))
+        for q in range(QUADS):
+            nc.scalar.dma_start(
+                out=v_sc_last[32 * q : 32 * q + 4, :].bitcast(I32),
+                in_=v_sc[32 * q + 4 : 32 * q + 8, :].bitcast(I32),
+            )
+        w1_w = held("w1_w", [P, PASSES * 2 * H], U8)
+        nc.vector.tensor_copy(
+            out=w1_w[:].rearrange("p (a t m b) -> p a t m b", a=PASSES, t=PACK, b=2),
+            in_=w1_raw[:].rearrange("p (a m t b) -> p a t m b", a=PASSES, t=PACK, b=2),
+        )
+        w3_w = held("w3_w", [P, PASSES * H], I32)
+        nc.vector.tensor_copy(
+            out=w3_w[:].rearrange("p (a t m) -> p a m t", a=PASSES, t=PACK),
+            in_=w3_raw[:].rearrange("p (a m t) -> p a m t", a=PASSES, t=PACK),
+        )
+        w13_sc = held("w13_sc", [P, PASSES * H], U8)
+
+        w2_w = held("w2_w", [P, PASSES * H], U32)
+        w2_sc = held("w2_sc", [P, PASSES * H], U8)
+        w2_bf = [held("w2_bf%d" % a, [P, PACK * H], BF16) for a in range(PASSES)]
+        for a in range(PASSES):
+            nc.scalar.copy(
+                out=w2_bf[a][:].rearrange("p (t m j) -> p m j t", t=PACK, j=PACK),
+                in_=w2_raw[a][:].rearrange("p j (m t) -> p m j t", t=PACK),
+            )
+
+        x0_sb = [keep.tile([P, T2], F32, name="x0_%d" % i, tag="wide%d" % i, align_bytes=64) for i in range(NT)]
+        for i in range(NT):
+            nc.sync.dma_start(out=x0_sb[i][:], in_=x0[P * i : P * (i + 1), :])
+
+        def quantize_w2(a):
+            cols = slice(H * a, H * (a + 1))
+            nc.vector.quantize_mx(out=w2_w[:, cols].bitcast(FP8X4), scales=w2_sc[:, cols], in_=w2_bf[a][:])
+
+        gather_words(0, 0)
+        quantize_w2(0)
+        gather_words(0, 1)
+        nc.vector.tensor_copy(
+            out=w13_sc[:].rearrange("p (a t m) -> p a t m", a=PASSES, t=PACK),
+            in_=w13_sc_raw[:].rearrange("p (a m t) -> p a t m", a=PASSES, t=PACK),
+        )
+        gather_words(1, 0)
+        quantize_w2(1)
+        gather_words(1, 1)
+
+        def mx_pass(acc, a, words, word_cols, dtype, scales, v_planes, u):
+            t, h = UNITS[u]
+            c0 = H * a + P * t
+            nc.tensor.matmul_mx(
+                out=acc[:],
+                lhsT=words[:, word_cols * c0 : word_cols * (c0 + P)].bitcast(dtype),
+                lhsT_scale=scales[:, c0 : c0 + P],
+                rhs=v_w[a][h][:].bitcast(FP8X4),
+                rhs_scale=v_planes[a][:, BANK * h : BANK * (h + 1)],
+                start=(a == 0),
+                stop=(a == PASSES - 1),
+            )
+
+        a_sb, b_ps, c_ps, c_sb, low, h_sb = {}, {}, {}, {}, {}, {}
+
+        def pass_a(acc, a, u):
+            mx_pass(acc, a, w1_w, 2, FP4X4, w13_sc[:, :], (v_sc[:, :], v_sc_last[:, :]), u)
+
+        def pass_b(acc, a, u):
+            mx_pass(acc, a, w2_w, 1, FP8X4, w2_sc[:, :], (v_sc[:, :], v_sc[4:P, :]), u)
+
+        def pass_c(acc, a, u):
+            mx_pass(acc, a, w3_w, 1, FP8X4, w13_sc[4:P, :], (v_sc[:, :], v_sc[4:P, :]), u)
+
+        def weights_of(t, cols):
+            return wgs_first[:, cols] if t == 0 else wgs_rest[:, t - 1, cols]
+
+        a_ps = {}
+
+        def open_a(u):
+            a_ps[u] = psum.tile([P, BANK], F32, name="acc_a", tag="bank_a", bufs=2)
+
+        def open_b(u):
+            b_ps[u] = psum.tile([P, BANK], F32, name="acc_b", tag="bank_b", bufs=3)
+
+        def open_c(u):
+            c_ps[u] = psum.tile([P, BANK], F32, name="acc_c", tag="bank_c", bufs=3)
+
+        def empty_a(u):
+            a_sb[u] = held("a_sb%d" % u, [P, BANK], F32)
+            nc.scalar.copy(out=a_sb[u][:], in_=a_ps[u][:])
+
+        def product_a(u):
+            open_a(u)
+            for a in range(PASSES):
+                pass_a(a_ps[u], a, u)
+            empty_a(u)
+
+        def product_b(u):
+            open_b(u)
+            for a in range(PASSES):
+                pass_b(b_ps[u], a, u)
+
+        def product_c(u):
+            open_c(u)
+            for a in range(PASSES):
+                pass_c(c_ps[u], a, u)
+
+        def smaller(u):
+            if u == 2:
+                pair = keep.tile([P, S], F32, name="low_pair", tag="first", align_bytes=64)
+                low[2], low[3] = pair[:, 0:BANK], pair[:, BANK:S]
+            elif u != 3:
+                single = ring.tile([P, BANK], F32, name="low", bufs=4)
+                low[u] = single[:]
+            nc.vector.tensor_tensor(low[u], b_ps[u][:], a_sb[u][:], MIN)
+
+        def exposure(u):
+            t, h = UNITS[u]
+            if h == 0:
+                h_sb[t] = ring.tile([P, S], F32, name="h_sb", bufs=2)
+            nc.vector.tensor_tensor(h_sb[t][:, BANK * h : BANK * (h + 1)], c_ps[u][:], low[u], MULT)
+
+        page_bf = [held("page_bf%d" % c, [P, WIDTHS[c], PACK], BF16) for c in range(CHUNKS)]
+
+        def place(t, c):
+            if c < NARROW and t >= 2:
+                nc.vector.tensor_copy(out=page_bf[c][:, :, t], in_=page[t][:, SPANS[c]])
+            else:
+                nc.scalar.copy(out=page_bf[c][:, :, t], in_=page[t][:, SPANS[c]])
+
+        def scatter(t):
+            nc.vector.tensor_tensor(page[t][:].indirect(scatter_list[:]), h_sb[t][:], weights_of(t, slice(0, S)), MULT)
+            nc.sync.dma_start(out=page_out[t], in_=page[t][:])
+
+        w5_bf = held("w5_bf", [P, N * PACK], BF16)
+        w5_w = held("w5_w", [P, N], U32)
+        w5_sc = held("w5_sc", [P, N], U8)
+
+        for a in range(PASSES):
+            for u in range(HALVES):
+                if a == 0:
+                    open_a(u)
+                    open_b(u)
+                    open_c(u)
+                pass_a(a_ps[u], a, u)
+                pass_b(b_ps[u], a, u)
+                pass_c(c_ps[u], a, u)
+                if a == PASSES - 1:
+                    empty_a(u)
+        smaller(0)
+        smaller(1)
+        exposure(0)
+        exposure(1)
+        for u in range(HALVES, 2 * HALVES):
+            product_a(u)
+            product_b(u)
+            product_c(u)
+        for u in range(2 * HALVES, len(UNITS)):
+            product_a(u)
+        for t in range(PACK):
+            u = HALVES * (t + 1)
+            if 0 < t < PACK - 1:
+                product_b(u)
+                product_c(u)
+                smaller(u)
+                product_b(u + 1)
+                product_c(u + 1)
+            scatter(t)
+            if t == 0:
+                smaller(u)
+            if t + 1 < PACK:
+                smaller(u + 1)
+                exposure(u)
+                exposure(u + 1)
+            if t == 0:
+                nc.scalar.copy(
+                    out=w5_bf[:].rearrange("p (c i j) -> p c j i", i=PACK, j=PACK),
+                    in_=w5_raw[:].rearrange("p j (c i) -> p c j i", i=PACK),
+                )
+            if t == 1:
+                for c0, c1 in ((0, 256), (256, N)):
+                    nc.vector.quantize_mx(
+                        out=w5_w[:, c0:c1].bitcast(FP8X4),
+                        scales=w5_sc[:, c0:c1],
+                        in_=w5_bf[:, PACK * c0 : PACK * c1],
+                    )
+            if t < PACK - 1:
+                for c in range(CHUNKS):
+                    place(t, c)
+
+        page_w = held("page_w", [P, T2], U32)
+        page_sc = held("page_sc", [P, T2], U8)
+        codes_out = out_2[0].rearrange("p m t -> p (m t)").bitcast(I32)
+
+        def quantize_page(c):
+            cols = SPANS[c]
+            nc.vector.quantize_mx(
+                out=page_w[:, cols].bitcast(FP8X4),
+                scales=page_sc[:, cols],
+                in_=page_bf[c][:].rearrange("p m t -> p (m t)"),
+            )
+
+        steps = [(c, i) for c in range(CHUNKS) for i in range(NT)]
+        e_ps, gate, kept = {}, {}, {}
+
+        def scores(s):
+            c, i = steps[s]
+            cols = SPANS[c]
+            wide = slice(0, WIDTHS[c])
+            d_ps = psum.tile([P, BANK], F32, name="acc_d", tag="bank_a", bufs=2)
+            nc.tensor.matmul_mx(
+                out=d_ps[:, wide],
+                lhsT=w4_w[:, 2 * P * i : 2 * P * (i + 1)].bitcast(FP4X4),
+                lhsT_scale=w4_sc[:, P * i : P * (i + 1)],
+                rhs=page_w[:, cols].bitcast(FP8X4),
+                rhs_scale=page_sc[:, cols],
+                start=True,
+                stop=True,
+            )
+            e_ps[s] = psum.tile([P, BANK], F32, name="acc_e", tag="bank_b" if s % 2 == 0 else "bank_c", bufs=3)
+            nc.tensor.matmul_mx(
+                out=e_ps[s][:, wide],
+                lhsT=w5_w[:, P * i : P * (i + 1)].bitcast(FP8X4),
+                lhsT_scale=w5_sc[:, P * i : P * (i + 1)],
+                rhs=page_w[:, cols].bitcast(FP8X4),
+                rhs_scale=page_sc[:, cols],
+                start=True,
+                stop=True,
+            )
+            gate[s] = ring.tile([P, BANK], F32, name="gate", tag="low", bufs=4)
+            nc.scalar.activation(gate[s][:, wide], d_ps[:, wide], SIGMOID)
+
+        def keep_part(s):
+            c, i = steps[s]
+            wide = slice(0, WIDTHS[c])
+            kept[s] = ring.tile([P, BANK], F32, name="kept")
+            nc.vector.tensor_tensor(kept[s][:, wide], gate[s][:, wide], x0_sb[i][:, SPANS[c]], MULT)
+
+        def finish(s):
+            c, i = steps[s]
+            y = ring.tile([P, BANK], F32, name="y", bufs=4)
+            wide = slice(0, WIDTHS[c])
+            nc.vector.tensor_tensor(y[:, wide], e_ps[s][:, wide], kept[s][:, wide], ADD)
+            nc.sync.dma_start(out=out_0[P * i : P * (i + 1), SPANS[c]], in_=y[:, wide])
+
+        place(PACK - 1, 0)
+        place(PACK - 1, 2)
+        place(PACK - 1, 1)
+        quantize_page(0)
+        quantize_page(1)
+        for s in range(len(steps)):
+            c, i = steps[s]
+            scores(s)
+            if i == NT - 1 and c + 3 < CHUNKS:
+                place(PACK - 1, c + 3)
+            keep_part(s)
+            if s > 0:
+                finish(s - 1)
+            if i == 0 and c + 2 < CHUNKS:
+                quantize_page(c + 2)
+                if c + 2 == CHUNKS - 1:
+                    nc.sync.dma_start(out=codes_out, in_=page_w[:].bitcast(I32))
+                    for q in range(QUADS):
+                        nc.sync.dma_start(
+                            out=out_3[0, 4 * q : 4 * q + 4, :].bitcast(I32),
+                            in_=page_sc[32 * q : 32 * q + 4, :].bitcast(I32),
+                        )
+        finish(len(steps) - 1)

@@ -20,18 +20,26 @@ SIGMOID = mybir.ActivationFunctionType.Sigmoid
 
 P = 128
 PACK = 4
-PASSES = K // (P * PACK)
+K_PASS = P * PACK
+PASSES = K // K_PASS
 BANK = 512
 HALVES = S // BANK
 LIST_COLS = BANK // 16
 UNITS = [(t, h) for t in range(PACK) for h in range(HALVES)]
-EDGES = (0, 256, 512, 1024, 1536, 2048)
+QUADS = 4
+QUAD_ROWS = 4
+QUAD_ORDER = (0, 2, 1, 3)
+SHIFT_ROWS = 32 * (QUADS - 1) + QUAD_ROWS
+ROW_TILES = N // P
+GROUPS = T2 // BANK
+
+EDGES = (0, BANK // 2, BANK, 2 * BANK, 3 * BANK, 4 * BANK)
 CHUNKS = len(EDGES) - 1
 SPANS = [slice(EDGES[c], EDGES[c + 1]) for c in range(CHUNKS)]
 WIDTHS = [EDGES[c + 1] - EDGES[c] for c in range(CHUNKS)]
-NARROW = 2
-NT = N // P
-QUADS = 4
+PLACE_AFTER = {(2, 0): 3, (2, ROW_TILES - 1): 4}
+QUANTIZE_AFTER = {(2, 1): 3, (3, 0): 4}
+GATE_BUFS = 4
 
 
 def tile_list_cable_inspection_ledger_kernel(
@@ -41,133 +49,144 @@ def tile_list_cable_inspection_ledger_kernel(
     nc = tc.nc
     with ExitStack() as ctx:
         keep = ctx.enter_context(tc.tile_pool(name="keep", bufs=1))
-        ring = ctx.enter_context(tc.tile_pool(name="ring", bufs=3))
+        ring = ctx.enter_context(tc.tile_pool(name="ring", bufs=GATE_BUFS))
         psum = ctx.enter_context(tc.psum_pool(name="psum", bufs=1))
 
-        def held(name, shape, dtype):
-            return keep.tile(shape, dtype, name=name, align_bytes=64)
+        def held(name, shape, dtype, slot=None):
+            return keep.tile(shape, dtype, name=name, tag=slot or name, align_bytes=64)
+
+        def bank(name, slot):
+            return psum.tile([P, BANK], F32, name=name, tag=slot)
 
         tab_sc = held("tab_sc", [P, T], U8)
         v_sc = held("v_sc", [P, S], U8)
         v_sc_last = held("v_sc_last", [P, S], U8)
-        warm = held("warm", [P, 16], F32)
+        zero = held("zero", [P, 16], F32)
         w13_sc_raw = held("w13_sc_raw", [P, PASSES * H], U8)
         w4_sc = held("w4_sc", [P, N], U8)
         nc.vector.memset(tab_sc[:].bitcast(I32), 0)
         nc.gpsimd.memset(w13_sc_raw[:].bitcast(I32), 0)
         nc.gpsimd.memset(w4_sc[:].bitcast(I32), 0)
         nc.gpsimd.memset(v_sc_last[:].bitcast(I32), 0)
-        nc.gpsimd.memset(warm[:, 0:8], 0.0)
-        nc.scalar.activation(warm[:, 8:9], warm[:, 0:1], SIGMOID)
+        nc.gpsimd.memset(zero[:, 0:8], -256.0)
+        nc.scalar.activation(zero[:, 8:9], zero[:, 0:1], SIGMOID)
 
-        def load_scale_rows(queue, plane, first_row, src):
+        def load_scale_rows(plane, first_row, src):
             for q in range(QUADS):
                 row = 32 * q + first_row
-                queue.dma_start(
-                    out=plane[row : row + 4, :].bitcast(I32).rearrange("r (a y) -> r a y", a=src.shape[0]),
-                    in_=src[:, 4 * q : 4 * q + 4, :].rearrange("a r y -> r a y").bitcast(I32),
+                nc.sync.dma_start(
+                    out=plane[row : row + QUAD_ROWS, :].bitcast(I32).rearrange("r (a y) -> r a y", a=src.shape[0]),
+                    in_=src[:, QUAD_ROWS * q : QUAD_ROWS * (q + 1), :].rearrange("a r y -> r a y").bitcast(I32),
                 )
 
-        load_scale_rows(nc.gpsimd, w13_sc_raw, 0, w1_scales)
-
         gather_list = held("gather_list", [P, S // 16], U16)
-        nc.sync.dma_start(gather_list[:], offs)
+        w1_raw = held("w1_raw", [P, PASSES * 2 * H], U8)
         w3_raw = held("w3_raw", [P, PASSES * H], I32)
+        w2_raw = [held("w2_raw%d" % a, [P, PACK, H], F32, "wide%d" % a) for a in range(PASSES)]
+        tab_w = [held("tab_w%d" % a, [P, T], U32) for a in range(PASSES)]
+
+        def load_w2(a):
+            rows = w2[K_PASS * a : K_PASS * (a + 1), :]
+            nc.sync.dma_start(out=w2_raw[a][:], in_=rows.rearrange("(p j) y -> p j y", j=PACK))
+
+        def load_table(a):
+            nc.sync.dma_start(out=tab_w[a][:].bitcast(I32), in_=tab_words[a].rearrange("p t i -> p (t i)").bitcast(I32))
+
+        nc.sync.dma_start(gather_list[:], offs)
         nc.sync.dma_start(
             out=w3_raw[:].rearrange("p (a y) -> p a y", a=PASSES),
             in_=w3_words.rearrange("a p y i -> p a (y i)").bitcast(I32),
         )
         for q in range(QUADS):
             nc.sync.dma_start(
-                out=tab_sc[32 * q : 32 * q + 4 * PASSES, :].bitcast(I32),
-                in_=tab_scales[:, 4 * q : 4 * q + 4, :].bitcast(I32),
+                out=tab_sc[32 * q : 32 * q + QUAD_ROWS * PASSES, :].bitcast(I32),
+                in_=tab_scales[:, QUAD_ROWS * q : QUAD_ROWS * (q + 1), :].bitcast(I32),
             )
-        w1_raw = held("w1_raw", [P, PASSES * 2 * H], U8)
+        load_table(0)
         nc.sync.dma_start(
             out=w1_raw[:].bitcast(I32).rearrange("p (a y) -> p a y", a=PASSES),
             in_=w1_words.rearrange("a p y -> p a y").bitcast(I32),
         )
-        w2_raw = [keep.tile([P, PACK, H], F32, name="w2_raw%d" % a, tag="wide%d" % a, align_bytes=64) for a in range(PASSES)]
-        tab_w = [held("tab_w%d" % a, [P, T], U32) for a in range(PASSES)]
-        for a in range(PASSES):
-            nc.sync.dma_start(out=w2_raw[a][:], in_=w2[512 * a : 512 * (a + 1), :].rearrange("(p j) y -> p j y", j=PACK))
-            if a == PASSES - 1:
-                load_scale_rows(nc.sync, w13_sc_raw, 4, w3_scales)
-            nc.sync.dma_start(out=tab_w[a][:].bitcast(I32), in_=tab_words[a].rearrange("p t i -> p (t i)").bitcast(I32))
+        load_scale_rows(w13_sc_raw, QUAD_ROWS, w3_scales)
+        load_w2(0)
+        load_scale_rows(w13_sc_raw, 0, w1_scales)
+        nc.vector.tensor_copy(v_sc[:], tab_sc[:].indirect(gather_list[:]))
+        nc.sync.dma_start(
+            out=v_sc_last[0:SHIFT_ROWS, :].bitcast(I32),
+            in_=v_sc[QUAD_ROWS : QUAD_ROWS + SHIFT_ROWS, :].bitcast(I32),
+        )
+        load_table(1)
+        load_w2(1)
         scatter_list = held("scatter_list", [P, S // 16], U16)
         nc.sync.dma_start(scatter_list[:], offs2)
 
         wgs_rows = wgs.rearrange("(i t) j -> i t j", t=PACK)
-        wgs_first = keep.tile([P, S], F32, name="wgs_first", tag="first", align_bytes=64)
-        wgs_rest = held("wgs_rest", [P, PACK - 1, S], F32)
+        wgs_sb = [held("wgs%d" % t, [P, S], F32) for t in range(PACK)]
         page_in = page0.rearrange("(p t) m -> t p m", t=PACK)
         page_out = out_1.rearrange("(p t) m -> t p m", t=PACK)
         page = [held("page%d" % t, [P, T2], F32) for t in range(PACK)]
-        for q in (0, 2, 1, 3):
-            nc.sync.dma_start(out=wgs_first[32 * q : 32 * (q + 1), :], in_=wgs_rows[:, 0, :])
-        nc.sync.dma_start(out=page[0][:], in_=page_in[0])
-        for q in (0, 2, 1, 3):
-            nc.sync.dma_start(out=wgs_rest[32 * q : 32 * (q + 1), :, :], in_=wgs_rows[:, 1:PACK, :])
-        nc.sync.dma_start(out=page[1][:], in_=page_in[1])
-        w5_raw = held("w5_raw", [P, PACK, N], F32)
-        nc.sync.dma_start(out=w5_raw[:], in_=w5.rearrange("(p j) n -> p j n", j=PACK))
-        w4_w = held("w4_w", [P, 2 * N], U8)
-        nc.sync.dma_start(out=w4_w[:].bitcast(I32), in_=w4_words[0].bitcast(I32))
-        load_scale_rows(nc.sync, w4_sc, 0, w4_scales)
-        for t in range(2, PACK):
+
+        def load_slice(t):
+            for q in QUAD_ORDER:
+                nc.sync.dma_start(out=wgs_sb[t][32 * q : 32 * (q + 1), :], in_=wgs_rows[:, t, :])
             nc.sync.dma_start(out=page[t][:], in_=page_in[t])
 
+        load_slice(0)
+        w5_raw = held("w5_raw", [P, PACK, N], F32)
+        nc.sync.dma_start(out=w5_raw[:], in_=w5.rearrange("(p j) n -> p j n", j=PACK))
+        load_slice(1)
+        w4_w = held("w4_w", [P, 2 * N], U8)
+        nc.sync.dma_start(out=w4_w[:].bitcast(I32), in_=w4_words[0].bitcast(I32))
+        load_scale_rows(w4_sc, 0, w4_scales)
+        load_slice(2)
+
         v_w = [[held("v_w%d%d" % (a, h), [P, BANK], U32) for h in range(HALVES)] for a in range(PASSES)]
+        w1_w = held("w1_w", [P, PASSES * 2 * H], U8)
+        w3_w = held("w3_w", [P, PASSES * H], I32)
+        w13_sc = held("w13_sc", [P, PASSES * H], U8)
+        w2_w = held("w2_w", [P, PASSES * H], U32)
+        w2_sc = held("w2_sc", [P, PASSES * H], U8)
+        w2_bf = [held("w2_bf%d" % a, [P, PACK * H], BF16) for a in range(PASSES)]
 
         def gather_words(a, h):
             part = gather_list[:, LIST_COLS * h : LIST_COLS * (h + 1)]
             nc.vector.tensor_copy(v_w[a][h][:], tab_w[a][:].indirect(part))
 
-        nc.vector.tensor_copy(v_sc[:], tab_sc[:].indirect(gather_list[:]))
-        for q in range(QUADS):
-            nc.scalar.dma_start(
-                out=v_sc_last[32 * q : 32 * q + 4, :].bitcast(I32),
-                in_=v_sc[32 * q + 4 : 32 * q + 8, :].bitcast(I32),
+        def quantize(words, scales, cols, values):
+            nc.vector.quantize_mx(out=words[:, cols].bitcast(FP8X4), scales=scales[:, cols], in_=values)
+
+        def quantize_w2(a):
+            nc.vector.tensor_copy(
+                out=w2_bf[a][:].rearrange("p (t m j) -> p m j t", t=PACK, j=PACK),
+                in_=w2_raw[a][:].rearrange("p j (m t) -> p m j t", t=PACK),
             )
-        w1_w = held("w1_w", [P, PASSES * 2 * H], U8)
-        nc.vector.tensor_copy(
-            out=w1_w[:].rearrange("p (a t m b) -> p a t m b", a=PASSES, t=PACK, b=2),
-            in_=w1_raw[:].rearrange("p (a m t b) -> p a t m b", a=PASSES, t=PACK, b=2),
-        )
-        w3_w = held("w3_w", [P, PASSES * H], I32)
+            quantize(w2_w, w2_sc, slice(H * a, H * (a + 1)), w2_bf[a][:])
+
         nc.vector.tensor_copy(
             out=w3_w[:].rearrange("p (a t m) -> p a m t", a=PASSES, t=PACK),
             in_=w3_raw[:].rearrange("p (a m t) -> p a m t", a=PASSES, t=PACK),
         )
-        w13_sc = held("w13_sc", [P, PASSES * H], U8)
-
-        w2_w = held("w2_w", [P, PASSES * H], U32)
-        w2_sc = held("w2_sc", [P, PASSES * H], U8)
-        w2_bf = [held("w2_bf%d" % a, [P, PACK * H], BF16) for a in range(PASSES)]
-        for a in range(PASSES):
-            nc.scalar.copy(
-                out=w2_bf[a][:].rearrange("p (t m j) -> p m j t", t=PACK, j=PACK),
-                in_=w2_raw[a][:].rearrange("p j (m t) -> p m j t", t=PACK),
-            )
-
-        x0_sb = [keep.tile([P, T2], F32, name="x0_%d" % i, tag="wide%d" % i, align_bytes=64) for i in range(NT)]
-        for i in range(NT):
-            nc.sync.dma_start(out=x0_sb[i][:], in_=x0[P * i : P * (i + 1), :])
-
-        def quantize_w2(a):
-            cols = slice(H * a, H * (a + 1))
-            nc.vector.quantize_mx(out=w2_w[:, cols].bitcast(FP8X4), scales=w2_sc[:, cols], in_=w2_bf[a][:])
-
-        gather_words(0, 0)
+        for h in range(HALVES):
+            gather_words(0, h)
+        nc.vector.tensor_copy(
+            out=w1_w[:].rearrange("p (a t m b) -> p a t m b", a=PASSES, t=PACK, b=2),
+            in_=w1_raw[:].rearrange("p (a m t b) -> p a t m b", a=PASSES, t=PACK, b=2),
+        )
         quantize_w2(0)
-        gather_words(0, 1)
         nc.vector.tensor_copy(
             out=w13_sc[:].rearrange("p (a t m) -> p a t m", a=PASSES, t=PACK),
             in_=w13_sc_raw[:].rearrange("p (a m t) -> p a t m", a=PASSES, t=PACK),
         )
-        gather_words(1, 0)
+        for h in range(HALVES):
+            gather_words(1, h)
         quantize_w2(1)
-        gather_words(1, 1)
+
+        x0_sb = [held("x0_%d" % i, [P, T2], F32, "wide%d" % i) for i in range(ROW_TILES)]
+        for i in range(ROW_TILES):
+            nc.sync.dma_start(out=x0_sb[i][:], in_=x0[P * i : P * (i + 1), :])
+        load_slice(3)
+
+        a_ps, b_ps, c_ps, a_sb, low, h_sb = {}, {}, {}, {}, {}, {}
 
         def mx_pass(acc, a, words, word_cols, dtype, scales, v_planes, u):
             t, h = UNITS[u]
@@ -182,30 +201,25 @@ def tile_list_cable_inspection_ledger_kernel(
                 stop=(a == PASSES - 1),
             )
 
-        a_sb, b_ps, c_ps, c_sb, low, h_sb = {}, {}, {}, {}, {}, {}
+        packed_planes = (v_sc[:, :], v_sc[QUAD_ROWS:P, :])
 
-        def pass_a(acc, a, u):
-            mx_pass(acc, a, w1_w, 2, FP4X4, w13_sc[:, :], (v_sc[:, :], v_sc_last[:, :]), u)
+        def pass_a(a, u):
+            mx_pass(a_ps[u], a, w1_w, 2, FP4X4, w13_sc[:, :], (v_sc[:, :], v_sc_last[:, :]), u)
 
-        def pass_b(acc, a, u):
-            mx_pass(acc, a, w2_w, 1, FP8X4, w2_sc[:, :], (v_sc[:, :], v_sc[4:P, :]), u)
+        def pass_b(a, u):
+            mx_pass(b_ps[u], a, w2_w, 1, FP8X4, w2_sc[:, :], packed_planes, u)
 
-        def pass_c(acc, a, u):
-            mx_pass(acc, a, w3_w, 1, FP8X4, w13_sc[4:P, :], (v_sc[:, :], v_sc[4:P, :]), u)
-
-        def weights_of(t, cols):
-            return wgs_first[:, cols] if t == 0 else wgs_rest[:, t - 1, cols]
-
-        a_ps = {}
+        def pass_c(a, u):
+            mx_pass(c_ps[u], a, w3_w, 1, FP8X4, w13_sc[QUAD_ROWS:P, :], packed_planes, u)
 
         def open_a(u):
-            a_ps[u] = psum.tile([P, BANK], F32, name="acc_a", tag="bank_a", bufs=2)
+            a_ps[u] = bank("acc_a", "a%d" % u if u < HALVES else "b%d" % (u % HALVES))
 
         def open_b(u):
-            b_ps[u] = psum.tile([P, BANK], F32, name="acc_b", tag="bank_b", bufs=3)
+            b_ps[u] = bank("acc_b", "b%d" % u if u < HALVES else ("x", "y", "a0")[(u - HALVES) % 3])
 
         def open_c(u):
-            c_ps[u] = psum.tile([P, BANK], F32, name="acc_c", tag="bank_c", bufs=3)
+            c_ps[u] = bank("acc_c", "c%d" % (u % HALVES))
 
         def empty_a(u):
             a_sb[u] = held("a_sb%d" % u, [P, BANK], F32)
@@ -214,122 +228,123 @@ def tile_list_cable_inspection_ledger_kernel(
         def product_a(u):
             open_a(u)
             for a in range(PASSES):
-                pass_a(a_ps[u], a, u)
+                pass_a(a, u)
             empty_a(u)
 
-        def product_b(u):
+        def products_bc(u):
             open_b(u)
             for a in range(PASSES):
-                pass_b(b_ps[u], a, u)
-
-        def product_c(u):
+                pass_b(a, u)
             open_c(u)
             for a in range(PASSES):
-                pass_c(c_ps[u], a, u)
+                pass_c(a, u)
 
         def smaller(u):
-            if u == 2:
-                pair = keep.tile([P, S], F32, name="low_pair", tag="first", align_bytes=64)
-                low[2], low[3] = pair[:, 0:BANK], pair[:, BANK:S]
-            elif u != 3:
-                single = ring.tile([P, BANK], F32, name="low", bufs=4)
-                low[u] = single[:]
-            nc.vector.tensor_tensor(low[u], b_ps[u][:], a_sb[u][:], MIN)
+            slot = "low1" if u == 1 else ("low0", "wgs0")[u % HALVES]
+            low[u] = held("low%d" % u, [P, BANK], F32, slot)
+            nc.vector.tensor_tensor(low[u][:], b_ps[u][:], a_sb[u][:], MIN)
 
         def exposure(u):
             t, h = UNITS[u]
             if h == 0:
-                h_sb[t] = ring.tile([P, S], F32, name="h_sb", bufs=2)
-            nc.vector.tensor_tensor(h_sb[t][:, BANK * h : BANK * (h + 1)], c_ps[u][:], low[u], MULT)
-
-        page_bf = [held("page_bf%d" % c, [P, WIDTHS[c], PACK], BF16) for c in range(CHUNKS)]
-
-        def place(t, c):
-            if c < NARROW and t >= 2:
-                nc.vector.tensor_copy(out=page_bf[c][:, :, t], in_=page[t][:, SPANS[c]])
-            else:
-                nc.scalar.copy(out=page_bf[c][:, :, t], in_=page[t][:, SPANS[c]])
+                h_sb[t] = held("h_sb%d" % t, [P, S], F32, "h_sb")
+            nc.vector.tensor_tensor(h_sb[t][:, BANK * h : BANK * (h + 1)], c_ps[u][:], low[u][:], MULT)
 
         def scatter(t):
-            nc.vector.tensor_tensor(page[t][:].indirect(scatter_list[:]), h_sb[t][:], weights_of(t, slice(0, S)), MULT)
+            nc.vector.tensor_tensor(page[t][:].indirect(scatter_list[:]), h_sb[t][:], wgs_sb[t][:], MULT)
             nc.sync.dma_start(out=page_out[t], in_=page[t][:])
 
-        w5_bf = held("w5_bf", [P, N * PACK], BF16)
-        w5_w = held("w5_w", [P, N], U32)
+        page_bf = {}
+        page_bf_slots = ("w1_w", "v_sc_last", "a_sb3", "a_sb4")
+
+        def place(t, cols):
+            g = cols.start // BANK
+            if g not in page_bf:
+                page_bf[g] = held("page_bf%d" % g, [P, BANK, PACK], BF16, page_bf_slots[g])
+            out = page_bf[g][:, cols.start - BANK * g : cols.stop - BANK * g, t]
+            if g == 0 and t >= 2:
+                nc.vector.tensor_copy(out=out, in_=page[t][:, cols])
+            else:
+                nc.scalar.copy(out=out, in_=page[t][:, cols])
+
+        def place_group(t, g):
+            place(t, slice(BANK * g, BANK * (g + 1)))
+
         w5_sc = held("w5_sc", [P, N], U8)
 
-        for a in range(PASSES):
-            for u in range(HALVES):
-                if a == 0:
-                    open_a(u)
-                    open_b(u)
-                    open_c(u)
-                pass_a(a_ps[u], a, u)
-                pass_b(b_ps[u], a, u)
-                pass_c(c_ps[u], a, u)
-                if a == PASSES - 1:
-                    empty_a(u)
-        smaller(0)
-        smaller(1)
-        exposure(0)
-        exposure(1)
+        for u in range(HALVES):
+            open_a(u)
+            open_b(u)
+            open_c(u)
+            pass_b(0, u)
+            pass_a(0, u)
+            pass_c(0, u)
+        for u in range(HALVES):
+            pass_a(1, u)
+            empty_a(u)
+            pass_c(1, u)
+        for u in range(HALVES):
+            pass_b(1, u)
+        for u in range(HALVES):
+            smaller(u)
+        for u in range(HALVES):
+            exposure(u)
         for u in range(HALVES, 2 * HALVES):
             product_a(u)
-            product_b(u)
-            product_c(u)
+        products_bc(HALVES)
         for u in range(2 * HALVES, len(UNITS)):
             product_a(u)
+
         for t in range(PACK):
             u = HALVES * (t + 1)
-            if 0 < t < PACK - 1:
-                product_b(u)
-                product_c(u)
+            if t + 1 < PACK:
+                if t > 0:
+                    products_bc(u)
                 smaller(u)
-                product_b(u + 1)
-                product_c(u + 1)
+                products_bc(u + 1)
             scatter(t)
             if t == 0:
-                smaller(u)
-            if t + 1 < PACK:
-                smaller(u + 1)
-                exposure(u)
-                exposure(u + 1)
-            if t == 0:
+                w5_bf = held("w5_bf", [P, N * PACK], BF16, "low1")
                 nc.scalar.copy(
                     out=w5_bf[:].rearrange("p (c i j) -> p c j i", i=PACK, j=PACK),
                     in_=w5_raw[:].rearrange("p j (c i) -> p c j i", i=PACK),
                 )
+            if t + 1 < PACK:
+                smaller(u + 1)
+                exposure(u)
+                exposure(u + 1)
+            if t == 2:
+                w5_w = held("w5_w", [P, N], U32, "a_sb6")
+                for cols in (slice(0, 2 * P), slice(2 * P, N)):
+                    quantize(w5_w, w5_sc, cols, w5_bf[:, PACK * cols.start : PACK * cols.stop])
             if t == 1:
-                for c0, c1 in ((0, 256), (256, N)):
-                    nc.vector.quantize_mx(
-                        out=w5_w[:, c0:c1].bitcast(FP8X4),
-                        scales=w5_sc[:, c0:c1],
-                        in_=w5_bf[:, PACK * c0 : PACK * c1],
-                    )
+                place_group(0, GROUPS - 1)
             if t < PACK - 1:
-                for c in range(CHUNKS):
-                    place(t, c)
+                for g in range(GROUPS - 1 if t == 0 else GROUPS):
+                    place_group(t, g)
 
+        bias_cell = {c: page_bf[SPANS[c].start // BANK][:, 0, PACK - 1 : PACK] for c in PLACE_AFTER.values()}
+        for cell in bias_cell.values():
+            nc.scalar.copy(out=cell, in_=zero[:, 8:9])
         page_w = held("page_w", [P, T2], U32)
         page_sc = held("page_sc", [P, T2], U8)
         codes_out = out_2[0].rearrange("p m t -> p (m t)").bitcast(I32)
 
         def quantize_page(c):
             cols = SPANS[c]
-            nc.vector.quantize_mx(
-                out=page_w[:, cols].bitcast(FP8X4),
-                scales=page_sc[:, cols],
-                in_=page_bf[c][:].rearrange("p m t -> p (m t)"),
-            )
+            first = PACK * (cols.start % BANK)
+            values = page_bf[cols.start // BANK][:].rearrange("p m t -> p (m t)")
+            quantize(page_w, page_sc, cols, values[:, first : first + PACK * WIDTHS[c]])
+            nc.sync.dma_start(out=codes_out[:, cols], in_=page_w[:, cols].bitcast(I32))
 
-        steps = [(c, i) for c in range(CHUNKS) for i in range(NT)]
-        e_ps, gate, kept = {}, {}, {}
+        steps = [(c, i) for c in range(CHUNKS) for i in range(ROW_TILES)]
+        e_ps, gate = {}, {}
 
         def scores(s):
             c, i = steps[s]
             cols = SPANS[c]
             wide = slice(0, WIDTHS[c])
-            d_ps = psum.tile([P, BANK], F32, name="acc_d", tag="bank_a", bufs=2)
+            d_ps = bank("acc_d", ("c0", "c1", "a1")[s % 3])
             nc.tensor.matmul_mx(
                 out=d_ps[:, wide],
                 lhsT=w4_w[:, 2 * P * i : 2 * P * (i + 1)].bitcast(FP4X4),
@@ -339,7 +354,7 @@ def tile_list_cable_inspection_ledger_kernel(
                 start=True,
                 stop=True,
             )
-            e_ps[s] = psum.tile([P, BANK], F32, name="acc_e", tag="bank_b" if s % 2 == 0 else "bank_c", bufs=3)
+            e_ps[s] = bank("acc_e", ("b0", "b1", "x", "y", "a0")[s % 5])
             nc.tensor.matmul_mx(
                 out=e_ps[s][:, wide],
                 lhsT=w5_w[:, P * i : P * (i + 1)].bitcast(FP8X4),
@@ -349,42 +364,46 @@ def tile_list_cable_inspection_ledger_kernel(
                 start=True,
                 stop=True,
             )
-            gate[s] = ring.tile([P, BANK], F32, name="gate", tag="low", bufs=4)
-            nc.scalar.activation(gate[s][:, wide], d_ps[:, wide], SIGMOID)
+            gate[s] = ring.tile([P, BANK], F32, name="gate")
+            if (c, i) in PLACE_AFTER:
+                nc.scalar.activation(gate[s][:, wide], d_ps[:, wide], SIGMOID, bias=bias_cell[PLACE_AFTER[c, i]])
+            else:
+                nc.scalar.activation(gate[s][:, wide], d_ps[:, wide], SIGMOID)
 
         def keep_part(s):
             c, i = steps[s]
-            wide = slice(0, WIDTHS[c])
-            kept[s] = ring.tile([P, BANK], F32, name="kept")
-            nc.vector.tensor_tensor(kept[s][:, wide], gate[s][:, wide], x0_sb[i][:, SPANS[c]], MULT)
+            y = x0_sb[i][:, SPANS[c]]
+            nc.vector.tensor_tensor(y, gate[s][:, 0 : WIDTHS[c]], y, MULT)
 
         def finish(s):
             c, i = steps[s]
-            y = ring.tile([P, BANK], F32, name="y", bufs=4)
-            wide = slice(0, WIDTHS[c])
-            nc.vector.tensor_tensor(y[:, wide], e_ps[s][:, wide], kept[s][:, wide], ADD)
-            nc.sync.dma_start(out=out_0[P * i : P * (i + 1), SPANS[c]], in_=y[:, wide])
+            y = x0_sb[i][:, SPANS[c]]
+            nc.vector.tensor_tensor(y, e_ps[s][:, 0 : WIDTHS[c]], y, ADD)
+            if c > 0:
+                cols = slice(0 if c == 1 else SPANS[c].start, SPANS[c].stop)
+                nc.sync.dma_start(out=out_0[P * i : P * (i + 1), cols], in_=x0_sb[i][:, cols])
 
-        place(PACK - 1, 0)
-        place(PACK - 1, 2)
-        place(PACK - 1, 1)
+        place(PACK - 1, SPANS[0])
+        place(PACK - 1, SPANS[2])
+        place(PACK - 1, SPANS[1])
         quantize_page(0)
         quantize_page(1)
         for s in range(len(steps)):
             c, i = steps[s]
             scores(s)
-            if i == NT - 1 and c + 3 < CHUNKS:
-                place(PACK - 1, c + 3)
+            if (c, i) in PLACE_AFTER:
+                place(PACK - 1, SPANS[PLACE_AFTER[c, i]])
             keep_part(s)
             if s > 0:
                 finish(s - 1)
-            if i == 0 and c + 2 < CHUNKS:
-                quantize_page(c + 2)
-                if c + 2 == CHUNKS - 1:
-                    nc.sync.dma_start(out=codes_out, in_=page_w[:].bitcast(I32))
+            if (c, i) == (0, 1):
+                quantize_page(2)
+            if (c, i) in QUANTIZE_AFTER:
+                quantize_page(QUANTIZE_AFTER[c, i])
+                if QUANTIZE_AFTER[c, i] == CHUNKS - 1:
                     for q in range(QUADS):
                         nc.sync.dma_start(
-                            out=out_3[0, 4 * q : 4 * q + 4, :].bitcast(I32),
-                            in_=page_sc[32 * q : 32 * q + 4, :].bitcast(I32),
+                            out=out_3[0, QUAD_ROWS * q : QUAD_ROWS * (q + 1), :].bitcast(I32),
+                            in_=page_sc[32 * q : 32 * q + QUAD_ROWS, :].bitcast(I32),
                         )
         finish(len(steps) - 1)

@@ -94,8 +94,8 @@ def tile_list_cable_inspection_ledger_kernel(
 
         nc.sync.dma_start(gather_list[:], offs)
         nc.sync.dma_start(
-            out=w3_raw[:].rearrange("p (a y) -> p a y", a=PASSES),
-            in_=w3_words.rearrange("a p y i -> p a (y i)").bitcast(I32),
+            out=w1_raw[:].bitcast(I32).rearrange("p (a y) -> p a y", a=PASSES),
+            in_=w1_words.rearrange("a p y -> p a y").bitcast(I32),
         )
         for q in range(QUADS):
             nc.sync.dma_start(
@@ -103,10 +103,6 @@ def tile_list_cable_inspection_ledger_kernel(
                 in_=tab_scales[:, QUAD_ROWS * q : QUAD_ROWS * (q + 1), :].bitcast(I32),
             )
         load_table(0)
-        nc.sync.dma_start(
-            out=w1_raw[:].bitcast(I32).rearrange("p (a y) -> p a y", a=PASSES),
-            in_=w1_words.rearrange("a p y -> p a y").bitcast(I32),
-        )
         load_scale_rows(w13_sc_raw, QUAD_ROWS, w3_scales)
         load_w2(0)
         load_scale_rows(w13_sc_raw, 0, w1_scales)
@@ -119,6 +115,10 @@ def tile_list_cable_inspection_ledger_kernel(
         load_w2(1)
         scatter_list = held("scatter_list", [P, S // 16], U16)
         nc.sync.dma_start(scatter_list[:], offs2)
+        nc.sync.dma_start(
+            out=w3_raw[:].rearrange("p (a y) -> p a y", a=PASSES),
+            in_=w3_words.rearrange("a p y i -> p a (y i)").bitcast(I32),
+        )
 
         wgs_rows = wgs.rearrange("(i t) j -> i t j", t=PACK)
         wgs_sb = [held("wgs%d" % t, [P, S], F32) for t in range(PACK)]
@@ -157,21 +157,17 @@ def tile_list_cable_inspection_ledger_kernel(
 
         def quantize_w2(a):
             nc.vector.tensor_copy(
-                out=w2_bf[a][:].rearrange("p (t m j) -> p m j t", t=PACK, j=PACK),
-                in_=w2_raw[a][:].rearrange("p j (m t) -> p m j t", t=PACK),
+                out=w2_bf[a][:].rearrange("p (t m j) -> p m t j", t=PACK, j=PACK),
+                in_=w2_raw[a][:].rearrange("p j (m t) -> p m t j", t=PACK),
             )
             quantize(w2_w, w2_sc, slice(H * a, H * (a + 1)), w2_bf[a][:])
 
         nc.vector.tensor_copy(
-            out=w3_w[:].rearrange("p (a t m) -> p a m t", a=PASSES, t=PACK),
-            in_=w3_raw[:].rearrange("p (a m t) -> p a m t", a=PASSES, t=PACK),
-        )
-        for h in range(HALVES):
-            gather_words(0, h)
-        nc.vector.tensor_copy(
             out=w1_w[:].rearrange("p (a t m b) -> p a t m b", a=PASSES, t=PACK, b=2),
             in_=w1_raw[:].rearrange("p (a m t b) -> p a t m b", a=PASSES, t=PACK, b=2),
         )
+        for h in range(HALVES):
+            gather_words(0, h)
         quantize_w2(0)
         nc.vector.tensor_copy(
             out=w13_sc[:].rearrange("p (a t m) -> p a t m", a=PASSES, t=PACK),
@@ -180,6 +176,10 @@ def tile_list_cable_inspection_ledger_kernel(
         for h in range(HALVES):
             gather_words(1, h)
         quantize_w2(1)
+        nc.vector.tensor_copy(
+            out=w3_w[:].rearrange("p (a t m) -> p a m t", a=PASSES, t=PACK),
+            in_=w3_raw[:].rearrange("p (a m t) -> p a m t", a=PASSES, t=PACK),
+        )
 
         x0_sb = [held("x0_%d" % i, [P, T2], F32, "wide%d" % i) for i in range(ROW_TILES)]
         for i in range(ROW_TILES):
@@ -213,10 +213,10 @@ def tile_list_cable_inspection_ledger_kernel(
             mx_pass(c_ps[u], a, w3_w, 1, FP8X4, w13_sc[QUAD_ROWS:P, :], packed_planes, u)
 
         def open_a(u):
-            a_ps[u] = bank("acc_a", "a%d" % u if u < HALVES else "b%d" % (u % HALVES))
+            a_ps[u] = bank("acc_a", "%s%d" % ("a" if u < 2 * HALVES else "b", u % HALVES))
 
         def open_b(u):
-            b_ps[u] = bank("acc_b", "b%d" % u if u < HALVES else ("x", "y", "a0")[(u - HALVES) % 3])
+            b_ps[u] = bank("acc_b", "b%d" % u if u < HALVES else ("x", "y")[u % HALVES])
 
         def open_c(u):
             c_ps[u] = bank("acc_c", "c%d" % (u % HALVES))
@@ -275,16 +275,17 @@ def tile_list_cable_inspection_ledger_kernel(
         for u in range(HALVES):
             open_a(u)
             open_b(u)
-            open_c(u)
             pass_b(0, u)
             pass_a(0, u)
-            pass_c(0, u)
         for u in range(HALVES):
             pass_a(1, u)
             empty_a(u)
-            pass_c(1, u)
         for u in range(HALVES):
             pass_b(1, u)
+        for u in range(HALVES):
+            open_c(u)
+            for a in range(PASSES):
+                pass_c(a, u)
         for u in range(HALVES):
             smaller(u)
         for u in range(HALVES):
@@ -340,35 +341,33 @@ def tile_list_cable_inspection_ledger_kernel(
         steps = [(c, i) for c in range(CHUNKS) for i in range(ROW_TILES)]
         e_ps, gate = {}, {}
 
-        def scores(s):
+        def page_product(acc, words, word_cols, dtype, scales, s):
             c, i = steps[s]
-            cols = SPANS[c]
+            nc.tensor.matmul_mx(
+                out=acc[:, 0 : WIDTHS[c]],
+                lhsT=words[:, word_cols * P * i : word_cols * P * (i + 1)].bitcast(dtype),
+                lhsT_scale=scales[:, P * i : P * (i + 1)],
+                rhs=page_w[:, SPANS[c]].bitcast(FP8X4),
+                rhs_scale=page_sc[:, SPANS[c]],
+                start=True,
+                stop=True,
+            )
+
+        def gate_scores(s):
+            c, i = steps[s]
             wide = slice(0, WIDTHS[c])
             d_ps = bank("acc_d", ("c0", "c1", "a1")[s % 3])
-            nc.tensor.matmul_mx(
-                out=d_ps[:, wide],
-                lhsT=w4_w[:, 2 * P * i : 2 * P * (i + 1)].bitcast(FP4X4),
-                lhsT_scale=w4_sc[:, P * i : P * (i + 1)],
-                rhs=page_w[:, cols].bitcast(FP8X4),
-                rhs_scale=page_sc[:, cols],
-                start=True,
-                stop=True,
-            )
-            e_ps[s] = bank("acc_e", ("b0", "b1", "x", "y", "a0")[s % 5])
-            nc.tensor.matmul_mx(
-                out=e_ps[s][:, wide],
-                lhsT=w5_w[:, P * i : P * (i + 1)].bitcast(FP8X4),
-                lhsT_scale=w5_sc[:, P * i : P * (i + 1)],
-                rhs=page_w[:, cols].bitcast(FP8X4),
-                rhs_scale=page_sc[:, cols],
-                start=True,
-                stop=True,
-            )
+            page_product(d_ps, w4_w, 2, FP4X4, w4_sc, s)
             gate[s] = ring.tile([P, BANK], F32, name="gate")
             if (c, i) in PLACE_AFTER:
                 nc.scalar.activation(gate[s][:, wide], d_ps[:, wide], SIGMOID, bias=bias_cell[PLACE_AFTER[c, i]])
+                place(PACK - 1, SPANS[PLACE_AFTER[c, i]])
             else:
                 nc.scalar.activation(gate[s][:, wide], d_ps[:, wide], SIGMOID)
+
+        def new_scores(s):
+            e_ps[s] = bank("acc_e", ("b0", "b1", "x", "y", "a0")[s % 5])
+            page_product(e_ps[s], w5_w, 1, FP8X4, w5_sc, s)
 
         def keep_part(s):
             c, i = steps[s]
@@ -390,9 +389,10 @@ def tile_list_cable_inspection_ledger_kernel(
         quantize_page(1)
         for s in range(len(steps)):
             c, i = steps[s]
-            scores(s)
-            if (c, i) in PLACE_AFTER:
-                place(PACK - 1, SPANS[PLACE_AFTER[c, i]])
+            if i == 0:
+                for ahead in range(s, s + ROW_TILES):
+                    gate_scores(ahead)
+            new_scores(s)
             keep_part(s)
             if s > 0:
                 finish(s - 1)

@@ -37,8 +37,8 @@ EDGES = (0, BANK // 2, BANK, 2 * BANK, 3 * BANK, 4 * BANK)
 CHUNKS = len(EDGES) - 1
 SPANS = [slice(EDGES[c], EDGES[c + 1]) for c in range(CHUNKS)]
 WIDTHS = [EDGES[c + 1] - EDGES[c] for c in range(CHUNKS)]
-PLACE_AFTER = {(2, 0): 3, (2, ROW_TILES - 1): 4}
-QUANTIZE_AFTER = {(2, 1): 3, (3, 0): 4}
+FIRST_WIDE = 2
+PLACE_AFTER = {(FIRST_WIDE, 0): FIRST_WIDE + 1, (FIRST_WIDE, ROW_TILES - 1): FIRST_WIDE + 2}
 GATE_BUFS = 4
 
 
@@ -61,15 +61,15 @@ def tile_list_cable_inspection_ledger_kernel(
         tab_sc = held("tab_sc", [P, T], U8)
         v_sc = held("v_sc", [P, S], U8)
         v_sc_last = held("v_sc_last", [P, S], U8)
-        zero = held("zero", [P, 16], F32)
+        zero = held("zero", [P, 2], F32)
         w13_sc_raw = held("w13_sc_raw", [P, PASSES * H], U8)
         w4_sc = held("w4_sc", [P, N], U8)
         nc.vector.memset(tab_sc[:].bitcast(I32), 0)
         nc.gpsimd.memset(w13_sc_raw[:].bitcast(I32), 0)
         nc.gpsimd.memset(w4_sc[:].bitcast(I32), 0)
         nc.gpsimd.memset(v_sc_last[:].bitcast(I32), 0)
-        nc.gpsimd.memset(zero[:, 0:8], -256.0)
-        nc.scalar.activation(zero[:, 8:9], zero[:, 0:1], SIGMOID)
+        nc.gpsimd.memset(zero[:, 0:1], -256.0)
+        nc.scalar.activation(zero[:, 1:2], zero[:, 0:1], SIGMOID)
 
         def load_scale_rows(plane, first_row, src):
             for q in range(QUADS):
@@ -183,8 +183,9 @@ def tile_list_cable_inspection_ledger_kernel(
 
         x0_sb = [held("x0_%d" % i, [P, T2], F32, "wide%d" % i) for i in range(ROW_TILES)]
         for i in range(ROW_TILES):
+            if i == ROW_TILES - 1:
+                load_slice(3)
             nc.sync.dma_start(out=x0_sb[i][:], in_=x0[P * i : P * (i + 1), :])
-        load_slice(3)
 
         a_ps, b_ps, c_ps, a_sb, low, h_sb = {}, {}, {}, {}, {}, {}
 
@@ -239,16 +240,19 @@ def tile_list_cable_inspection_ledger_kernel(
             for a in range(PASSES):
                 pass_c(a, u)
 
+        low_slots = ("low0", "low1", "wgs0", "low0")
+
         def smaller(u):
-            slot = "low1" if u == 1 else ("low0", "wgs0")[u % HALVES]
-            low[u] = held("low%d" % u, [P, BANK], F32, slot)
-            nc.vector.tensor_tensor(low[u][:], b_ps[u][:], a_sb[u][:], MIN)
+            t, h = UNITS[u]
+            if h == 0:
+                low[t] = held("low%d" % t, [P, S], F32, low_slots[t])
+            nc.vector.tensor_tensor(low[t][:, BANK * h : BANK * (h + 1)], b_ps[u][:], a_sb[u][:], MIN)
 
         def exposure(u):
             t, h = UNITS[u]
             if h == 0:
-                h_sb[t] = held("h_sb%d" % t, [P, S], F32, "h_sb")
-            nc.vector.tensor_tensor(h_sb[t][:, BANK * h : BANK * (h + 1)], c_ps[u][:], low[u][:], MULT)
+                h_sb[t] = held("h_sb%d" % t, [P, S], F32, "h_sb%d" % (t % 2))
+            nc.vector.tensor_tensor(h_sb[t][:, BANK * h : BANK * (h + 1)], c_ps[u][:], low[t][:, BANK * h : BANK * (h + 1)], MULT)
 
         def scatter(t):
             nc.vector.tensor_tensor(page[t][:].indirect(scatter_list[:]), h_sb[t][:], wgs_sb[t][:], MULT)
@@ -292,30 +296,28 @@ def tile_list_cable_inspection_ledger_kernel(
             exposure(u)
         for u in range(HALVES, 2 * HALVES):
             product_a(u)
-        products_bc(HALVES)
-        for u in range(2 * HALVES, len(UNITS)):
-            product_a(u)
 
         for t in range(PACK):
             u = HALVES * (t + 1)
             if t + 1 < PACK:
-                if t > 0:
-                    products_bc(u)
+                products_bc(u)
                 smaller(u)
                 products_bc(u + 1)
+                smaller(u + 1)
+                exposure(u)
+                exposure(u + 1)
+            if t == 0:
+                for rest in range(2 * HALVES, len(UNITS)):
+                    product_a(rest)
             scatter(t)
             if t == 0:
-                w5_bf = held("w5_bf", [P, N * PACK], BF16, "low1")
+                w5_bf = held("w5_bf", [P, N * PACK], BF16, "a_sb2")
                 nc.scalar.copy(
                     out=w5_bf[:].rearrange("p (c i j) -> p c j i", i=PACK, j=PACK),
                     in_=w5_raw[:].rearrange("p j (c i) -> p c j i", i=PACK),
                 )
-            if t + 1 < PACK:
-                smaller(u + 1)
-                exposure(u)
-                exposure(u + 1)
             if t == 2:
-                w5_w = held("w5_w", [P, N], U32, "a_sb6")
+                w5_w = held("w5_w", [P, N], U32, "wgs1")
                 for cols in (slice(0, 2 * P), slice(2 * P, N)):
                     quantize(w5_w, w5_sc, cols, w5_bf[:, PACK * cols.start : PACK * cols.stop])
             if t == 1:
@@ -326,7 +328,7 @@ def tile_list_cable_inspection_ledger_kernel(
 
         bias_cell = {c: page_bf[SPANS[c].start // BANK][:, 0, PACK - 1 : PACK] for c in PLACE_AFTER.values()}
         for cell in bias_cell.values():
-            nc.scalar.copy(out=cell, in_=zero[:, 8:9])
+            nc.scalar.copy(out=cell, in_=zero[:, 1:2])
         page_w = held("page_w", [P, T2], U32)
         page_sc = held("page_sc", [P, T2], U8)
         codes_out = out_2[0].rearrange("p m t -> p (m t)").bitcast(I32)
@@ -356,7 +358,7 @@ def tile_list_cable_inspection_ledger_kernel(
         def gate_scores(s):
             c, i = steps[s]
             wide = slice(0, WIDTHS[c])
-            d_ps = bank("acc_d", ("c0", "c1", "a1")[s % 3])
+            d_ps = bank("acc_d", ("c0", "c1", "a1", "a0", "y")[s % 5])
             page_product(d_ps, w4_w, 2, FP4X4, w4_sc, s)
             gate[s] = ring.tile([P, BANK], F32, name="gate")
             if (c, i) in PLACE_AFTER:
@@ -366,7 +368,7 @@ def tile_list_cable_inspection_ledger_kernel(
                 nc.scalar.activation(gate[s][:, wide], d_ps[:, wide], SIGMOID)
 
         def new_scores(s):
-            e_ps[s] = bank("acc_e", ("b0", "b1", "x", "y", "a0")[s % 5])
+            e_ps[s] = bank("acc_e", ("b0", "b1", "x")[s % 3])
             page_product(e_ps[s], w5_w, 1, FP8X4, w5_sc, s)
 
         def keep_part(s):
@@ -383,7 +385,7 @@ def tile_list_cable_inspection_ledger_kernel(
                 nc.sync.dma_start(out=out_0[P * i : P * (i + 1), cols], in_=x0_sb[i][:, cols])
 
         place(PACK - 1, SPANS[0])
-        place(PACK - 1, SPANS[2])
+        place(PACK - 1, SPANS[FIRST_WIDE])
         place(PACK - 1, SPANS[1])
         quantize_page(0)
         quantize_page(1)
@@ -396,11 +398,12 @@ def tile_list_cable_inspection_ledger_kernel(
             keep_part(s)
             if s > 0:
                 finish(s - 1)
-            if (c, i) == (0, 1):
-                quantize_page(2)
-            if (c, i) in QUANTIZE_AFTER:
-                quantize_page(QUANTIZE_AFTER[c, i])
-                if QUANTIZE_AFTER[c, i] == CHUNKS - 1:
+            if s == 1:
+                quantize_page(FIRST_WIDE)
+            if s > 0 and steps[s - 1] in PLACE_AFTER:
+                later = PLACE_AFTER[steps[s - 1]]
+                quantize_page(later)
+                if later == CHUNKS - 1:
                     for q in range(QUADS):
                         nc.sync.dma_start(
                             out=out_3[0, QUAD_ROWS * q : QUAD_ROWS * (q + 1), :].bitcast(I32),

from contextlib import ExitStack

import concourse.mybir as mybir

K, H, N, T, S, T2 = 1024, 512, 384, 2048, 1024, 2048
FLOPS = 2 * (3 * K * H * S + 2 * H * N * T2)

F32 = mybir.dt.float32
BF16 = mybir.dt.bfloat16
I32 = mybir.dt.int32
U32 = mybir.dt.uint32
U16 = mybir.dt.uint16
U8 = mybir.dt.uint8
FP8X4 = mybir.dt.float8_e4m3fn_x4
FP4X4 = mybir.dt.float4_e2m1fn_x4
MULT = mybir.AluOpType.mult
MIN = mybir.AluOpType.min
ADD = mybir.AluOpType.add
SIGMOID = mybir.ActivationFunctionType.Sigmoid

P = 128
PACK = 4
K_PASS = P * PACK
PASSES = K // K_PASS
BANK = 512
HALVES = S // BANK
LIST_COLS = BANK // 16
UNITS = [(t, h) for t in range(PACK) for h in range(HALVES)]
QUADS = 4
QUAD_ROWS = 4
QUAD_ORDER = (0, 2, 1, 3)
SHIFT_ROWS = 32 * (QUADS - 1) + QUAD_ROWS
ROW_TILES = N // P
GROUPS = T2 // BANK

EDGES = (0, BANK // 2, BANK, 2 * BANK, 3 * BANK, 4 * BANK)
CHUNKS = len(EDGES) - 1
SPANS = [slice(EDGES[c], EDGES[c + 1]) for c in range(CHUNKS)]
WIDTHS = [EDGES[c + 1] - EDGES[c] for c in range(CHUNKS)]
FIRST_WIDE = 2
PLACE_AFTER = {(FIRST_WIDE, 0): FIRST_WIDE + 1, (FIRST_WIDE, ROW_TILES - 1): FIRST_WIDE + 2}
GATE_BUFS = 4


def tile_list_cable_inspection_ledger_kernel(
    tc, tab_words, tab_scales, offs, w1_words, w1_scales, w2, w3_words, w3_scales,
    page0, offs2, wgs, w4_words, w4_scales, w5, x0, out_0, out_1, out_2, out_3,
):
    nc = tc.nc
    with ExitStack() as ctx:
        keep = ctx.enter_context(tc.tile_pool(name="keep", bufs=1))
        ring = ctx.enter_context(tc.tile_pool(name="ring", bufs=GATE_BUFS))
        psum = ctx.enter_context(tc.psum_pool(name="psum", bufs=1))

        def held(name, shape, dtype, slot=None):
            return keep.tile(shape, dtype, name=name, tag=slot or name, align_bytes=64)

        def bank(name, slot):
            return psum.tile([P, BANK], F32, name=name, tag=slot)

        tab_sc = held("tab_sc", [P, T], U8)
        v_sc = held("v_sc", [P, S], U8)
        v_sc_last = held("v_sc_last", [P, S], U8)
        zero = held("zero", [P, 2], F32)
        w13_sc_raw = held("w13_sc_raw", [P, PASSES * H], U8)
        w4_sc = held("w4_sc", [P, N], U8)
        nc.vector.memset(tab_sc[:].bitcast(I32), 0)
        nc.gpsimd.memset(w13_sc_raw[:].bitcast(I32), 0)
        nc.gpsimd.memset(w4_sc[:].bitcast(I32), 0)
        nc.gpsimd.memset(v_sc_last[:].bitcast(I32), 0)
        nc.gpsimd.memset(zero[:, 0:1], -256.0)
        nc.scalar.activation(zero[:, 1:2], zero[:, 0:1], SIGMOID)

        def load_scale_rows(plane, first_row, src):
            for q in range(QUADS):
                row = 32 * q + first_row
                nc.sync.dma_start(
                    out=plane[row : row + QUAD_ROWS, :].bitcast(I32).rearrange("r (a y) -> r a y", a=src.shape[0]),
                    in_=src[:, QUAD_ROWS * q : QUAD_ROWS * (q + 1), :].rearrange("a r y -> r a y").bitcast(I32),
                )

        gather_list = held("gather_list", [P, S // 16], U16)
        w1_raw = held("w1_raw", [P, PASSES * 2 * H], U8)
        w3_raw = held("w3_raw", [P, PASSES * H], I32)
        w2_raw = [held("w2_raw%d" % a, [P, PACK, H], F32, "wide%d" % a) for a in range(PASSES)]
        tab_w = [held("tab_w%d" % a, [P, T], U32) for a in range(PASSES)]

        def load_w2(a):
            rows = w2[K_PASS * a : K_PASS * (a + 1), :]
            nc.sync.dma_start(out=w2_raw[a][:], in_=rows.rearrange("(p j) y -> p j y", j=PACK))

        def load_table(a):
            nc.sync.dma_start(out=tab_w[a][:].bitcast(I32), in_=tab_words[a].rearrange("p t i -> p (t i)").bitcast(I32))

        nc.sync.dma_start(gather_list[:], offs)
        nc.sync.dma_start(
            out=w1_raw[:].bitcast(I32).rearrange("p (a y) -> p a y", a=PASSES),
            in_=w1_words.rearrange("a p y -> p a y").bitcast(I32),
        )
        for q in range(QUADS):
            nc.sync.dma_start(
                out=tab_sc[32 * q : 32 * q + QUAD_ROWS * PASSES, :].bitcast(I32),
                in_=tab_scales[:, QUAD_ROWS * q : QUAD_ROWS * (q + 1), :].bitcast(I32),
            )
        load_table(0)
        load_scale_rows(w13_sc_raw, QUAD_ROWS, w3_scales)
        load_w2(0)
        load_scale_rows(w13_sc_raw, 0, w1_scales)
        nc.vector.tensor_copy(v_sc[:], tab_sc[:].indirect(gather_list[:]))
        nc.sync.dma_start(
            out=v_sc_last[0:SHIFT_ROWS, :].bitcast(I32),
            in_=v_sc[QUAD_ROWS : QUAD_ROWS + SHIFT_ROWS, :].bitcast(I32),
        )
        load_table(1)
        load_w2(1)
        scatter_list = held("scatter_list", [P, S // 16], U16)
        nc.sync.dma_start(scatter_list[:], offs2)
        nc.sync.dma_start(
            out=w3_raw[:].rearrange("p (a y) -> p a y", a=PASSES),
            in_=w3_words.rearrange("a p y i -> p a (y i)").bitcast(I32),
        )

        wgs_rows = wgs.rearrange("(i t) j -> i t j", t=PACK)
        wgs_sb = [held("wgs%d" % t, [P, S], F32) for t in range(PACK)]
        page_in = page0.rearrange("(p t) m -> t p m", t=PACK)
        page_out = out_1.rearrange("(p t) m -> t p m", t=PACK)
        page = [held("page%d" % t, [P, T2], F32) for t in range(PACK)]

        def load_slice(t):
            for q in QUAD_ORDER:
                nc.sync.dma_start(out=wgs_sb[t][32 * q : 32 * (q + 1), :], in_=wgs_rows[:, t, :])
            nc.sync.dma_start(out=page[t][:], in_=page_in[t])

        load_slice(0)
        w5_raw = held("w5_raw", [P, PACK, N], F32)
        nc.sync.dma_start(out=w5_raw[:], in_=w5.rearrange("(p j) n -> p j n", j=PACK))
        load_slice(1)
        w4_w = held("w4_w", [P, 2 * N], U8)
        nc.sync.dma_start(out=w4_w[:].bitcast(I32), in_=w4_words[0].bitcast(I32))
        load_scale_rows(w4_sc, 0, w4_scales)
        load_slice(2)

        v_w = [[held("v_w%d%d" % (a, h), [P, BANK], U32) for h in range(HALVES)] for a in range(PASSES)]
        w1_w = held("w1_w", [P, PASSES * 2 * H], U8)
        w3_w = held("w3_w", [P, PASSES * H], I32)
        w13_sc = held("w13_sc", [P, PASSES * H], U8)
        w2_w = held("w2_w", [P, PASSES * H], U32)
        w2_sc = held("w2_sc", [P, PASSES * H], U8)
        w2_bf = [held("w2_bf%d" % a, [P, PACK * H], BF16) for a in range(PASSES)]

        def gather_words(a, h):
            part = gather_list[:, LIST_COLS * h : LIST_COLS * (h + 1)]
            nc.vector.tensor_copy(v_w[a][h][:], tab_w[a][:].indirect(part))

        def quantize(words, scales, cols, values):
            nc.vector.quantize_mx(out=words[:, cols].bitcast(FP8X4), scales=scales[:, cols], in_=values)

        def quantize_w2(a):
            nc.vector.tensor_copy(
                out=w2_bf[a][:].rearrange("p (t m j) -> p m t j", t=PACK, j=PACK),
                in_=w2_raw[a][:].rearrange("p j (m t) -> p m t j", t=PACK),
            )
            quantize(w2_w, w2_sc, slice(H * a, H * (a + 1)), w2_bf[a][:])

        nc.vector.tensor_copy(
            out=w1_w[:].rearrange("p (a t m b) -> p a t m b", a=PASSES, t=PACK, b=2),
            in_=w1_raw[:].rearrange("p (a m t b) -> p a t m b", a=PASSES, t=PACK, b=2),
        )
        for h in range(HALVES):
            gather_words(0, h)
        quantize_w2(0)
        nc.vector.tensor_copy(
            out=w13_sc[:].rearrange("p (a t m) -> p a t m", a=PASSES, t=PACK),
            in_=w13_sc_raw[:].rearrange("p (a m t) -> p a t m", a=PASSES, t=PACK),
        )
        for h in range(HALVES):
            gather_words(1, h)
        quantize_w2(1)
        nc.vector.tensor_copy(
            out=w3_w[:].rearrange("p (a t m) -> p a m t", a=PASSES, t=PACK),
            in_=w3_raw[:].rearrange("p (a m t) -> p a m t", a=PASSES, t=PACK),
        )

        x0_sb = [held("x0_%d" % i, [P, T2], F32, "wide%d" % i) for i in range(ROW_TILES)]
        for i in range(ROW_TILES):
            if i == ROW_TILES - 1:
                load_slice(3)
            nc.sync.dma_start(out=x0_sb[i][:], in_=x0[P * i : P * (i + 1), :])

        a_ps, b_ps, c_ps, a_sb, low, h_sb = {}, {}, {}, {}, {}, {}

        def mx_pass(acc, a, words, word_cols, dtype, scales, v_planes, u):
            t, h = UNITS[u]
            c0 = H * a + P * t
            nc.tensor.matmul_mx(
                out=acc[:],
                lhsT=words[:, word_cols * c0 : word_cols * (c0 + P)].bitcast(dtype),
                lhsT_scale=scales[:, c0 : c0 + P],
                rhs=v_w[a][h][:].bitcast(FP8X4),
                rhs_scale=v_planes[a][:, BANK * h : BANK * (h + 1)],
                start=(a == 0),
                stop=(a == PASSES - 1),
            )

        packed_planes = (v_sc[:, :], v_sc[QUAD_ROWS:P, :])

        def pass_a(a, u):
            mx_pass(a_ps[u], a, w1_w, 2, FP4X4, w13_sc[:, :], (v_sc[:, :], v_sc_last[:, :]), u)

        def pass_b(a, u):
            mx_pass(b_ps[u], a, w2_w, 1, FP8X4, w2_sc[:, :], packed_planes, u)

        def pass_c(a, u):
            mx_pass(c_ps[u], a, w3_w, 1, FP8X4, w13_sc[QUAD_ROWS:P, :], packed_planes, u)

        def open_a(u):
            a_ps[u] = bank("acc_a", "%s%d" % ("a" if u < 2 * HALVES else "b", u % HALVES))

        def open_b(u):
            b_ps[u] = bank("acc_b", "b%d" % u if u < HALVES else ("x", "y")[u % HALVES])

        def open_c(u):
            c_ps[u] = bank("acc_c", "c%d" % (u % HALVES))

        def empty_a(u):
            a_sb[u] = held("a_sb%d" % u, [P, BANK], F32)
            nc.scalar.copy(out=a_sb[u][:], in_=a_ps[u][:])

        def product_a(u):
            open_a(u)
            for a in range(PASSES):
                pass_a(a, u)
            empty_a(u)

        def products_bc(u):
            open_b(u)
            for a in range(PASSES):
                pass_b(a, u)
            open_c(u)
            for a in range(PASSES):
                pass_c(a, u)

        low_slots = ("low0", "low1", "wgs0", "low0")

        def smaller(u):
            t, h = UNITS[u]
            if h == 0:
                low[t] = held("low%d" % t, [P, S], F32, low_slots[t])
            nc.vector.tensor_tensor(low[t][:, BANK * h : BANK * (h + 1)], b_ps[u][:], a_sb[u][:], MIN)

        def exposure(u):
            t, h = UNITS[u]
            if h == 0:
                h_sb[t] = held("h_sb%d" % t, [P, S], F32, "h_sb%d" % (t % 2))
            nc.vector.tensor_tensor(h_sb[t][:, BANK * h : BANK * (h + 1)], c_ps[u][:], low[t][:, BANK * h : BANK * (h + 1)], MULT)

        def scatter(t):
            nc.vector.tensor_tensor(page[t][:].indirect(scatter_list[:]), h_sb[t][:], wgs_sb[t][:], MULT)
            nc.sync.dma_start(out=page_out[t], in_=page[t][:])

        page_bf = {}
        page_bf_slots = ("w1_w", "v_sc_last", "a_sb3", "a_sb4")

        def place(t, cols):
            g = cols.start // BANK
            if g not in page_bf:
                page_bf[g] = held("page_bf%d" % g, [P, BANK, PACK], BF16, page_bf_slots[g])
            out = page_bf[g][:, cols.start - BANK * g : cols.stop - BANK * g, t]
            if g == 0 and t >= 2:
                nc.vector.tensor_copy(out=out, in_=page[t][:, cols])
            else:
                nc.scalar.copy(out=out, in_=page[t][:, cols])

        def place_group(t, g):
            place(t, slice(BANK * g, BANK * (g + 1)))

        w5_sc = held("w5_sc", [P, N], U8)

        for u in range(HALVES):
            open_a(u)
            open_b(u)
            pass_b(0, u)
            pass_a(0, u)
        for u in range(HALVES):
            pass_a(1, u)
            empty_a(u)
        for u in range(HALVES):
            pass_b(1, u)
        for u in range(HALVES):
            open_c(u)
            for a in range(PASSES):
                pass_c(a, u)
        for u in range(HALVES):
            smaller(u)
        for u in range(HALVES):
            exposure(u)
        for u in range(HALVES, 2 * HALVES):
            product_a(u)

        for t in range(PACK):
            u = HALVES * (t + 1)
            if t + 1 < PACK:
                products_bc(u)
                smaller(u)
                products_bc(u + 1)
                smaller(u + 1)
                exposure(u)
                exposure(u + 1)
            if t == 0:
                for rest in range(2 * HALVES, len(UNITS)):
                    product_a(rest)
            scatter(t)
            if t == 0:
                w5_bf = held("w5_bf", [P, N * PACK], BF16, "a_sb2")
                nc.scalar.copy(
                    out=w5_bf[:].rearrange("p (c i j) -> p c j i", i=PACK, j=PACK),
                    in_=w5_raw[:].rearrange("p j (c i) -> p c j i", i=PACK),
                )
            if t == 2:
                w5_w = held("w5_w", [P, N], U32, "wgs1")
                for cols in (slice(0, 2 * P), slice(2 * P, N)):
                    quantize(w5_w, w5_sc, cols, w5_bf[:, PACK * cols.start : PACK * cols.stop])
            if t == 1:
                place_group(0, GROUPS - 1)
            if t < PACK - 1:
                for g in range(GROUPS - 1 if t == 0 else GROUPS):
                    place_group(t, g)

        bias_cell = {c: page_bf[SPANS[c].start // BANK][:, 0, PACK - 1 : PACK] for c in PLACE_AFTER.values()}
        for cell in bias_cell.values():
            nc.scalar.copy(out=cell, in_=zero[:, 1:2])
        page_w = held("page_w", [P, T2], U32)
        page_sc = held("page_sc", [P, T2], U8)
        codes_out = out_2[0].rearrange("p m t -> p (m t)").bitcast(I32)

        def quantize_page(c):
            cols = SPANS[c]
            first = PACK * (cols.start % BANK)
            values = page_bf[cols.start // BANK][:].rearrange("p m t -> p (m t)")
            quantize(page_w, page_sc, cols, values[:, first : first + PACK * WIDTHS[c]])
            nc.sync.dma_start(out=codes_out[:, cols], in_=page_w[:, cols].bitcast(I32))

        steps = [(c, i) for c in range(CHUNKS) for i in range(ROW_TILES)]
        e_ps, gate = {}, {}

        def page_product(acc, words, word_cols, dtype, scales, s):
            c, i = steps[s]
            nc.tensor.matmul_mx(
                out=acc[:, 0 : WIDTHS[c]],
                lhsT=words[:, word_cols * P * i : word_cols * P * (i + 1)].bitcast(dtype),
                lhsT_scale=scales[:, P * i : P * (i + 1)],
                rhs=page_w[:, SPANS[c]].bitcast(FP8X4),
                rhs_scale=page_sc[:, SPANS[c]],
                start=True,
                stop=True,
            )

        def gate_scores(s):
            c, i = steps[s]
            wide = slice(0, WIDTHS[c])
            d_ps = bank("acc_d", ("c0", "c1", "a1", "a0", "y")[s % 5])
            page_product(d_ps, w4_w, 2, FP4X4, w4_sc, s)
            gate[s] = ring.tile([P, BANK], F32, name="gate")
            if (c, i) in PLACE_AFTER:
                nc.scalar.activation(gate[s][:, wide], d_ps[:, wide], SIGMOID, bias=bias_cell[PLACE_AFTER[c, i]])
                place(PACK - 1, SPANS[PLACE_AFTER[c, i]])
            else:
                nc.scalar.activation(gate[s][:, wide], d_ps[:, wide], SIGMOID)

        def new_scores(s):
            e_ps[s] = bank("acc_e", ("b0", "b1", "x")[s % 3])
            page_product(e_ps[s], w5_w, 1, FP8X4, w5_sc, s)

        def keep_part(s):
            c, i = steps[s]
            y = x0_sb[i][:, SPANS[c]]
            nc.vector.tensor_tensor(y, gate[s][:, 0 : WIDTHS[c]], y, MULT)

        def finish(s):
            c, i = steps[s]
            y = x0_sb[i][:, SPANS[c]]
            nc.vector.tensor_tensor(y, e_ps[s][:, 0 : WIDTHS[c]], y, ADD)
            if c > 0:
                cols = slice(0 if c == 1 else SPANS[c].start, SPANS[c].stop)
                nc.sync.dma_start(out=out_0[P * i : P * (i + 1), cols], in_=x0_sb[i][:, cols])

        place(PACK - 1, SPANS[0])
        place(PACK - 1, SPANS[FIRST_WIDE])
        place(PACK - 1, SPANS[1])
        quantize_page(0)
        quantize_page(1)
        for s in range(len(steps)):
            c, i = steps[s]
            if i == 0:
                for ahead in range(s, s + ROW_TILES):
                    gate_scores(ahead)
            new_scores(s)
            keep_part(s)
            if s > 0:
                finish(s - 1)
            if s == 1:
                quantize_page(FIRST_WIDE)
            if s > 0 and steps[s - 1] in PLACE_AFTER:
                later = PLACE_AFTER[steps[s - 1]]
                quantize_page(later)
                if later == CHUNKS - 1:
                    for q in range(QUADS):
                        nc.sync.dma_start(
                            out=out_3[0, QUAD_ROWS * q : QUAD_ROWS * (q + 1), :].bitcast(I32),
                            in_=page_sc[32 * q : 32 * q + QUAD_ROWS, :].bitcast(I32),
                        )
        finish(len(steps) - 1)
